import numpy as np
import ml_dtypes


def mxq(x, axis, fmt="e4m3"):
    dtype, down = {"e4m3": (ml_dtypes.float8_e4m3fn, 7), "e5m2": (ml_dtypes.float8_e5m2, 14)}[fmt]
    v = np.moveaxis(np.asarray(x, np.float32).astype(ml_dtypes.bfloat16).astype(np.float64), axis, -1)
    blocks = v.reshape(v.shape[:-1] + (-1, 32))
    amax = np.abs(blocks).max(-1, keepdims=True)
    byte = np.maximum(np.where(amax > 0, np.frexp(amax)[1] - 1 + 127, 0) - down, 1)
    scale = np.exp2(byte - 127.0)
    codes = (blocks / scale).astype(np.float32).astype(dtype).astype(np.float64)
    return np.moveaxis((codes * scale).reshape(v.shape), -1, axis)


WIDE = False


def mx_kscale(k):
    if not WIDE:
        return np.ones(k)
    levels = np.array([30, -30])
    if k % 512:
        return np.exp2(np.random.permutation(np.resize(levels, k // 32))).repeat(32)
    a = np.empty((k // 512, 16))
    for p in range(k // 512):
        a[p, :8] = np.random.permutation(np.resize(levels, 8))
        for g in range(8):
            far = levels[np.abs(levels - a[p, g]) >= 10]
            a[p, g + 8] = far[np.random.randint(len(far))]
    return np.exp2(a.ravel()).repeat(32)


BF16 = ml_dtypes.bfloat16


def bf(x):
    return np.asarray(x, np.float32).astype(BF16)


def f64(x):
    return np.asarray(x).astype(np.float64)


E2M1 = np.array([0.0, 0.5, 1.0, 1.5, 2.0, 3.0, 4.0, 6.0, -0.0, -0.5, -1.0, -1.5, -2.0, -3.0, -4.0, -6.0])


def pack_weight(w, fmt):
    k, n = w.shape
    w = f64(bf(w)).reshape(k // 32, 32, n)
    amax = np.abs(w).max(1)
    if fmt == "e4m3":
        byte = np.frexp(amax)[1] - 1 + 127 - 7
    else:
        mant, ex = np.frexp(amax / 6.0)
        byte = np.where(mant > 0.5, ex, ex - 1) + 127
    byte = np.clip(np.where(amax > 0, byte, 1), 1, 254)
    scaled = (w * np.exp2(127.0 - byte)[:, None, :]).reshape(k, n).astype(np.float32)
    by_word = np.ascontiguousarray(scaled.reshape(k // 512, 128, 4, n).transpose(0, 1, 3, 2))
    if fmt == "e4m3":
        words = by_word.astype(ml_dtypes.float8_e4m3fn).view(np.uint8)
    else:
        c = by_word.astype(ml_dtypes.float4_e2m1fn).view(np.uint8) & 0xF
        words = c[..., 0::2] | (c[..., 1::2] << 4)
    return np.ascontiguousarray(words), np.ascontiguousarray(byte.astype(np.uint8).reshape(k // 512, 16, n))


def unpack_weight(words, scales, fmt):
    g, p, n, _ = words.shape
    if fmt == "e4m3":
        vals = np.ascontiguousarray(words).view(ml_dtypes.float8_e4m3fn).astype(np.float64)
    else:
        nib = np.empty((g, p, n, 4), np.uint8)
        nib[..., 0::2] = words & 0xF
        nib[..., 1::2] = words >> 4
        vals = E2M1[nib]
    vals = vals * np.repeat(np.exp2(scales.astype(np.float64) - 127.0), 8, axis=1)[..., None]
    return vals.transpose(0, 1, 3, 2).reshape(g * 512, n)
def pack4(w):
    words, scales = pack_weight(w, "e2m1")
    return words.reshape(words.shape[0], 128, -1), scales


def unpack4(words, scales):
    return unpack_weight(words.reshape(words.shape[0], 128, -1, 2), scales, "e2m1")


M, P, C = 1024, 2048, 1024


def setup_inputs():
    s = mx_kscale(P)
    t = mx_kscale(C)
    x = bf(np.random.standard_normal((M, P)) * s)
    wa_words, wa_scales = pack4(np.random.standard_normal((P, C)) / np.sqrt(P) / s[:, None])
    return {"x": x,
            "wa_words": wa_words,
            "wa_scales": wa_scales,
            "ba": bf(0.4 * np.random.standard_normal(C)),
            "inv_step": bf((0.5 + np.random.random(C)) * t),
            "ws": bf(np.random.standard_normal((C, P)) / np.sqrt(C) / t[:, None]),
            "contrast": bf(0.5 + np.random.random(M)),
            "mean": bf(0.4 * np.random.standard_normal(P))}


def reference(x, wa_words, wa_scales, ba, inv_step, ws, contrast, mean):
    wa = unpack4(wa_words, wa_scales)
    y = mxq(f64(x), 1, "e4m3") @ wa
    z = (y + f64(ba)) * f64(inv_step)
    r = mxq(z, 1, "e5m2") @ mxq(f64(ws), 0, "e4m3")
    return r * f64(contrast)[:, None] + f64(mean)

@@ -1,0 +1,403 @@
+from contextlib import ExitStack
+
+import concourse.mybir as mybir
+from concourse.masks import make_identity
+
+M, PIX, C = 1024, 2048, 1024
+FLOPS = 2 * M * PIX * C * 2
+
+F32 = mybir.dt.float32
+BF16 = mybir.dt.bfloat16
+I32 = mybir.dt.int32
+U32 = mybir.dt.uint32
+U8 = mybir.dt.uint8
+E4M3 = mybir.dt.float8_e4m3fn_x4
+E5M2 = mybir.dt.float8_e5m2_x4
+E2M1 = mybir.dt.float4_e2m1fn_x4
+ALU = mybir.AluOpType
+ACT = mybir.ActivationFunctionType
+
+P = 128
+PACK = 4
+K_PASS = P * PACK
+N = 512
+X_PASSES = PIX // K_PASS
+Z_PASSES = C // K_PASS
+HALVES = M // N
+TILES = N // P
+OUT_CHUNKS = PIX // N
+WS_WIDTH = 2 * N
+BANKS = 8
+
+
+def tile_latent_patch_codec_s9_kernel(tc, x, wa_words, wa_scales, ba, inv_step, ws, contrast, mean, out):
+    nc = tc.nc
+    x_rows = x.rearrange("(p h j) k -> h p j k", h=HALVES, j=TILES)
+    out_rows = out.rearrange("(p h j) n -> h j p n", h=HALVES, j=TILES)
+    ws_rows = ws.rearrange("(G a t r) n -> G r a t n", G=Z_PASSES, t=PACK, r=4)
+
+    with ExitStack() as ctx:
+        keep = ctx.enter_context(tc.tile_pool(name="keep", bufs=1))
+        stage = ctx.enter_context(tc.tile_pool(name="stage", bufs=3))
+        psum = ctx.enter_context(tc.psum_pool(name="psum", bufs=1))
+        ctx.enter_context(tc.manual_schedule())
+
+        tiles = {}
+
+        def kept(key, shape, dtype):
+            tiles[key] = keep.tile(shape, dtype, name="k" + "x".join([str(part) for part in key]), align_bytes=64)
+            return tiles[key]
+
+        def staged(key, shape, dtype, bufs):
+            tiles[key] = stage.tile(shape, dtype, name="s" + "x".join([str(part) for part in key]), tag=key[0], bufs=bufs, align_bytes=64)
+            return tiles[key]
+
+        def bank(key, number):
+            tiles[key] = psum.tile([P, N], F32, name="b" + "x".join([str(part) for part in key]), tag="bank%d" % (number % BANKS))
+            return tiles[key]
+
+        def copy_on(engine, dst, src):
+            if engine == "scalar":
+                nc.scalar.copy(out=dst, in_=src)
+            else:
+                nc.vector.tensor_copy(out=dst, in_=src)
+
+        def load_x(h, g0, count):
+            raw = kept(("xraw", h, g0), [P, TILES, count * K_PASS], BF16)
+            nc.sync.dma_start(out=raw[:], in_=x_rows[h, :, :, g0 * K_PASS : (g0 + count) * K_PASS])
+            for g in range(g0, g0 + count):
+                tiles[("xwords", h, g)] = raw[:].bitcast(F32)[:, :, (g - g0) * 256 : (g - g0 + 1) * 256]
+
+        def load_wa(g):
+            raw = kept(("waraw", g), [P, C // 2], I32)
+            nc.sync.dma_start(out=raw[:], in_=wa_words[g].bitcast(I32))
+
+        def load_wa_scales():
+            raw = kept(("scraw",), [P, X_PASSES, C // 4], I32)
+            nc.vector.memset(raw[:], 0)
+            for q in range(4):
+                nc.sync.dma_start(out=raw[32 * q : 32 * q + 4, :, :],
+                                  in_=wa_scales[:, 4 * q : 4 * q + 4, :].rearrange("g r n -> r g n").bitcast(I32))
+
+        def load_ws(G, w):
+            raw = kept(("wsraw", G, w), [P, PACK, WS_WIDTH], BF16)
+            for r in range(4):
+                nc.sync.dma_start(out=raw[r:P:4, :, :], in_=ws_rows[G, r, :, :, w * WS_WIDTH : (w + 1) * WS_WIDTH])
+
+        def load_mean():
+            row = kept(("mean",), [P, PIX], BF16)
+            nc.sync.dma_start(out=row[:], in_=mean.partition_broadcast(P))
+
+        def load_channel_rows():
+            raw = kept(("chraw",), [P, Z_PASSES * P], BF16)
+            for i, vec in enumerate((ba, inv_step)):
+                nc.sync.dma_start(out=raw[PACK * i : PACK * (i + 1), :].rearrange("t (c r) -> t c r", r=4),
+                                  in_=vec.rearrange("(c t r) -> t c r", t=PACK, r=4))
+
+        def load_contrast():
+            gain = kept(("contrast",), [P, HALVES * TILES], BF16)
+            nc.sync.dma_start(out=gain[:], in_=contrast.rearrange("(p j) -> p j", p=P))
+
+        def widen_channel_rows():
+            nc.vector.tensor_copy(out=tiles[("chrows",)][0 : 2 * PACK, :], in_=tiles[("chraw",)][0 : 2 * PACK, :])
+
+        def turn_channel_rows(number):
+            acc = bank(("chT",), number)
+            for G in range(Z_PASSES):
+                nc.tensor.transpose(acc[:, G * P : (G + 1) * P], tiles[("chrows",)][:, G * P : (G + 1) * P], ident[:])
+
+        def read_channel_columns():
+            acc = tiles[("chT",)][:, 0 : Z_PASSES * P].rearrange("p (G c) -> p G c", G=Z_PASSES)
+            step = kept(("step",), [P, Z_PASSES, PACK], F32)
+            nc.vector.tensor_copy(out=step[:], in_=acc[:, :, PACK : 2 * PACK])
+            shift = kept(("shift",), [P, Z_PASSES, PACK], F32)
+            nc.vector.tensor_tensor(out=shift[:], in0=acc[:, :, 0:PACK], in1=step[:], op=ALU.mult)
+
+        def sort_wa(g):
+            codes = kept(("wa", g), [P, 2 * C], U8)
+            nc.vector.tensor_copy(
+                out=codes[:].bitcast(I32).rearrange("p (t c a e) -> p c t a e", t=PACK, a=2, e=2),
+                in_=tiles[("waraw", g)][:].rearrange("p (c a t e) -> p c t a e", t=PACK, a=2, e=2))
+
+        def sort_wa_scales(g0, count):
+            if g0 == 0:
+                kept(("wasc",), [P, X_PASSES * C], U8)
+            words = tiles[("wasc",)][:].bitcast(I32)[:, g0 * (C // 4) : (g0 + count) * (C // 4)]
+            nc.vector.tensor_copy(
+                out=words.rearrange("p (g t c i) -> p g c t i", g=count, t=PACK, i=4),
+                in_=tiles[("scraw",)][:, g0 : g0 + count, :].rearrange("p g (c i t) -> p g c t i", t=PACK, i=4))
+
+        def turn_x(h, g, number):
+            words = tiles[("xwords", h, g)]
+            for b in range(2):
+                acc = bank(("xT", h, g, b), number + b)
+                for jj in range(2):
+                    for u in range(2):
+                        s = 2 * jj + u
+                        nc.tensor.transpose(acc[:, s * P : (s + 1) * P], words[:, 2 * b + jj, u::2], ident[:])
+
+        def drain_x(h, g, b, engine):
+            if b == 0:
+                staged(("xg", h, g), [P, PACK * N], BF16, 3)
+            dst = tiles[("xg", h, g)][:].bitcast(F32)[:, b * N : (b + 1) * N].rearrange("p (j m u) -> p j m u", j=2, u=2)
+            copy_on(engine, dst, tiles[("xT", h, g, b)][:].rearrange("p (j u m) -> p j m u", j=2, u=2))
+
+        def quantize(key, src, fmt, parts=(0, 1)):
+            if parts[0] == 0:
+                kept(key + ("q",), [P, N], U32)
+                kept(key + ("s",), [P, N], U8)
+            lo, hi = parts[0] * (N // 2), (parts[-1] + 1) * (N // 2)
+            nc.vector.quantize_mx(out=tiles[key + ("q",)][:, lo:hi].bitcast(fmt), scales=tiles[key + ("s",)][:, lo:hi],
+                                  in_=src[:, PACK * lo : PACK * hi])
+
+        def quant_x(h, g):
+            quantize(("x", h, g), tiles[("xg", h, g)][:], E4M3)
+
+        def analysis_pass(h, G, t, g, number):
+            if g == 0:
+                bank(("y", h, G, t), number)
+            col = (t * Z_PASSES + G) * P
+            nc.tensor.matmul_mx(
+                out=tiles[("y", h, G, t)][:],
+                lhsT=tiles[("wa", g)][:, 2 * col : 2 * (col + P)].bitcast(E2M1),
+                lhsT_scale=tiles[("wasc",)][:, g * C + col : g * C + col + P],
+                rhs=tiles[("x", h, g, "q")][:].bitcast(E4M3),
+                rhs_scale=tiles[("x", h, g, "s")][:],
+                start=(g == 0), stop=(g == X_PASSES - 1))
+
+        def analysis(h, G, t, number):
+            for g in range(X_PASSES):
+                analysis_pass(h, G, t, g, number)
+
+        def drain_y(h, G, t, parts=(0, 1)):
+            if t == 0:
+                staged(("zrows", h, G), [P, PACK, N], BF16, 2)
+            cols = slice(parts[0] * (N // 2), (parts[-1] + 1) * (N // 2))
+            nc.scalar.activation(out=tiles[("zrows", h, G)][:, t, cols], in_=tiles[("y", h, G, t)][:, cols], func=ACT.Identity,
+                                 bias=tiles[("shift",)][:, G, t : t + 1], scale=tiles[("step",)][:, G, t : t + 1])
+
+        def weave(key, src, engine, parts):
+            if ("woven",) + key not in tiles:
+                staged(("woven",) + key, [P, PACK * N], BF16, 4)
+            cols = slice(parts[0] * (N // 2), (parts[-1] + 1) * (N // 2))
+            dst = tiles[("woven",) + key][:].rearrange("p (n t) -> p n t", t=PACK)[:, cols, :]
+            copy_on(engine, dst.rearrange("p (c i) t -> p c t i", i=4), src[:, :, cols].rearrange("p t (c i) -> p c t i", i=4))
+
+        def weave_z(h, G, engine, parts=(0, 1)):
+            weave(("z", h, G), tiles[("zrows", h, G)][:], engine, parts)
+
+        def quant_z(h, G, parts=(0, 1)):
+            quantize(("z", h, G), tiles[("woven", "z", h, G)][:], E5M2, parts)
+
+        def weave_ws(G, n, engine, parts=(0, 1)):
+            w, part = divmod(n, WS_WIDTH // N)
+            weave(("ws", G, n), tiles[("wsraw", G, w)][:, :, part * N : (part + 1) * N], engine, parts)
+
+        def quant_ws(G, n):
+            quantize(("ws", G, n), tiles[("woven", "ws", G, n)][:], E4M3)
+
+        def synthesis_pass(h, j, n, G, number):
+            if G == 0:
+                bank(("r", h, j, n), number)
+            nc.tensor.matmul_mx(
+                out=tiles[("r", h, j, n)][:],
+                lhsT=tiles[("z", h, G, "q")][:, j * P : (j + 1) * P].bitcast(E5M2),
+                lhsT_scale=tiles[("z", h, G, "s")][:, j * P : (j + 1) * P],
+                rhs=tiles[("ws", G, n, "q")][:].bitcast(E4M3),
+                rhs_scale=tiles[("ws", G, n, "s")][:],
+                start=(G == 0), stop=(G == Z_PASSES - 1))
+
+        def widen_contrast():
+            nc.vector.tensor_copy(out=kept(("gain",), [P, HALVES * TILES], F32)[:], in_=tiles[("contrast",)][:])
+
+        def finish(h, j, n, first, count, aside):
+            if n == first:
+                staged(("res", h, j, first), [P, count * N], F32, 6)
+            res = tiles[("res", h, j, first)][:, (n - first) * N : (n - first + 1) * N]
+            row = h * TILES + j
+            gain = tiles[("gain",)][:, row : row + 1]
+            shift = tiles[("mean",)][:, n * N : (n + 1) * N]
+            if aside:
+                nc.scalar.activation(out=res, in_=tiles[("r", h, j, n)][:], func=ACT.Copy, scale=gain)
+                nc.gpsimd.tensor_tensor(out=res, in0=res, in1=shift, op=ALU.add)
+            else:
+                nc.vector.scalar_tensor_tensor(out=res, in0=tiles[("r", h, j, n)][:], scalar=gain, in1=shift, op0=ALU.mult, op1=ALU.add)
+            if n == first + count - 1:
+                nc.sync.dma_start(out=out_rows[h, j, :, first * N : (first + count) * N], in_=tiles[("res", h, j, first)][:])
+
+        def synthesis(h, j, n, number, first=None, count=1, aside=False):
+            for G in range(Z_PASSES):
+                synthesis_pass(h, j, n, G, number)
+            finish(h, j, n, n if first is None else first, count, aside)
+
+        ident = kept(("ident",), [P, P], F32)
+        make_identity(nc, ident[:])
+
+        def make_warm_operands():
+            zeros = kept(("zeros",), [P, P], BF16)
+            codes = kept(("warmq",), [P, N + P], U32)
+            plane = kept(("warms",), [P, N + P], U8)
+            nc.vector.memset(zeros[:], 0.0)
+            nc.vector.memset(codes[:], 0)
+            nc.vector.memset(plane[:].bitcast(U32), 0)
+            nc.vector.quantize_mx(out=codes[:, 0:32].bitcast(E4M3), scales=plane[:, 0:32], in_=zeros[:])
+            nc.vector.quantize_mx(out=codes[:, N : N + 32].bitcast(E5M2), scales=plane[:, N : N + 32], in_=zeros[:])
+
+        def warm(count, first):
+            codes, plane = tiles[("warmq",)], tiles[("warms",)]
+            for i in range(count):
+                acc = bank(("warm", first + i), i % 4)
+                nc.tensor.matmul_mx(out=acc[:], lhsT=codes[:, N : N + P].bitcast(E5M2), lhsT_scale=plane[:, N : N + P],
+                                    rhs=codes[:, 0:N].bitcast(E4M3), rhs_scale=plane[:, 0:N], start=True, stop=True)
+
+        nc.gpsimd.memset(kept(("chrows",), [P, Z_PASSES * P], F32)[:], 0.0)
+        load_x(0, 0, 1)
+        load_wa_scales()
+        make_warm_operands()
+        load_wa(0)
+        load_x(0, 1, 1)
+        load_wa(1)
+        load_x(0, 2, 1)
+        load_channel_rows()
+        load_wa(2)
+        load_x(0, 3, 1)
+        load_wa(3)
+        load_ws(0, 0)
+        load_x(1, 0, 2)
+        load_ws(1, 0)
+        load_x(1, 2, 2)
+        load_contrast()
+        load_mean()
+        load_ws(0, 1)
+        load_ws(1, 1)
+
+        def drain_both(h, g, e0="scalar", e1="scalar"):
+            drain_x(h, g, 0, e0)
+            drain_x(h, g, 1, e1)
+
+        def wide(h, G, g, number):
+            for t in range(PACK):
+                analysis_pass(h, G, t, g, number + t)
+
+        warm(3, 0)
+        turn_x(0, 0, 4)
+        warm(2, 4)
+        sort_wa_scales(0, 1)
+        sort_wa(0)
+        drain_both(0, 0, "scalar", "vector")
+        turn_x(0, 1, 6)
+        quant_x(0, 0)
+        drain_both(0, 1)
+        sort_wa_scales(1, 3)
+        sort_wa(1)
+        wide(0, 0, 0, 0)
+        quant_x(0, 1)
+        turn_x(0, 2, 4)
+        drain_both(0, 2)
+        sort_wa(2)
+        widen_channel_rows()
+        wide(0, 0, 1, 0)
+        sort_wa(3)
+        quant_x(0, 2)
+        turn_x(0, 3, 6)
+        turn_channel_rows(4)
+        drain_both(0, 3)
+        weave_ws(0, 0, "vector", (0,))
+        wide(0, 0, 2, 0)
+        for g in range(3):
+            analysis_pass(0, 1, 0, g, 5)
+        quant_x(0, 3)
+        weave_ws(0, 0, "vector", (1,))
+        read_channel_columns()
+        wide(0, 0, 3, 0)
+        analysis_pass(0, 1, 0, 3, 5)
+        weave_ws(0, 1, "scalar", (0,))
+        weave_ws(0, 1, "vector", (1,))
+        quant_ws(0, 0)
+        for t in range(PACK):
+            drain_y(0, 0, t)
+        quant_ws(0, 1)
+        analysis(0, 1, 1, 6)
+        turn_x(1, 0, 7)
+        analysis(0, 1, 2, 4)
+        analysis(0, 1, 3, 1)
+        weave_ws(1, 0, "vector")
+        weave_z(0, 0, "vector")
+        drain_y(0, 1, 0)
+        drain_both(1, 0)
+        drain_y(0, 1, 1)
+        quant_ws(1, 0)
+        quant_x(1, 0)
+        quant_z(0, 0)
+        weave_ws(1, 1, "vector", (0,))
+        turn_x(1, 1, 2)
+        drain_y(0, 1, 2)
+        drain_y(0, 1, 3)
+        drain_both(1, 1)
+        wide(1, 0, 0, 4)
+        weave_z(0, 1, "vector")
+        quant_x(1, 1)
+        quant_z(0, 1)
+        weave_ws(1, 1, "scalar", (1,))
+        turn_x(1, 2, 0)
+        drain_both(1, 2)
+        wide(1, 0, 1, 4)
+        quant_ws(1, 1)
+        widen_contrast()
+        quant_x(1, 2)
+        weave_ws(0, 2, "vector")
+        weave_ws(1, 2, "scalar", (0,))
+        turn_x(1, 3, 2)
+        drain_both(1, 3)
+        synthesis(0, 0, 0, 0)
+        synthesis(0, 1, 0, 1)
+        wide(1, 0, 2, 4)
+        weave_ws(1, 2, "scalar", (1,))
+        quant_x(1, 3)
+        quant_ws(0, 2)
+        weave_ws(0, 3, "scalar")
+        synthesis(0, 2, 0, 2)
+        synthesis(0, 3, 0, 3)
+        wide(1, 0, 3, 4)
+        quant_ws(1, 2)
+        for t in range(PACK):
+            drain_y(1, 0, t)
+        synthesis(0, 0, 1, 0)
+        synthesis(0, 1, 1, 1)
+        quant_ws(0, 3)
+        synthesis(0, 2, 1, 2)
+        synthesis(0, 3, 1, 3)
+        weave_ws(1, 3, "scalar", (0,))
+        analysis(1, 1, 0, 4)
+        weave_z(1, 0, "vector")
+        drain_y(1, 1, 0)
+        weave_ws(1, 3, "scalar", (1,))
+        synthesis(0, 0, 2, 5)
+        quant_z(1, 0)
+        synthesis(0, 1, 2, 6)
+        analysis(1, 1, 1, 7)
+        drain_y(1, 1, 1)
+        synthesis(0, 2, 2, 0)
+        quant_ws(1, 3)
+        analysis(1, 1, 2, 1)
+        analysis(1, 1, 3, 2)
+        drain_y(1, 1, 2)
+        drain_y(1, 1, 3, (0,))
+        weave_z(1, 1, "scalar", (0,))
+        drain_y(1, 1, 3, (1,))
+        weave_z(1, 1, "scalar", (1,))
+        synthesis(0, 3, 2, 3)
+        synthesis(0, 0, 3, 4)
+        synthesis(0, 1, 3, 5)
+        quant_z(1, 1, (0,))
+        synthesis(0, 2, 3, 6)
+        synthesis(0, 3, 3, 7)
+        quant_z(1, 1, (1,))
+        number = 0
+        for j in range(TILES):
+            for n in range(OUT_CHUNKS):
+                if j == TILES - 1 and n >= 2:
+                    synthesis(1, j, n, number)
+                else:
+                    synthesis(1, j, n, number, first=n - n % 2, count=2, aside=False)
+                number = number + 1

@@ -85,33 +85,48 @@ def tile_latent_patch_codec_s9_kernel(tc, x, wa_words, wa_scales, ba, inv_step, 
                 nc.sync.dma_start(out=raw[r:P:4, :, :], in_=ws_rows[G, r, :, :, w * WS_WIDTH : (w + 1) * WS_WIDTH])
 
         def load_mean():
-            row = kept(("mean",), [P, PIX], BF16)
-            nc.sync.dma_start(out=row[:], in_=mean.partition_broadcast(P))
+            rows = kept(("meanrows",), [P, PIX // P], BF16)
+            nc.sync.dma_start(out=rows[:], in_=mean.rearrange("(n w) -> n w", n=P))
 
         def load_channel_rows():
-            raw = kept(("chraw",), [P, Z_PASSES * P], BF16)
+            raw = kept(("chraw",), [P, K_PASS], BF16)
             for i, vec in enumerate((ba, inv_step)):
-                nc.sync.dma_start(out=raw[PACK * i : PACK * (i + 1), :].rearrange("t (c r) -> t c r", r=4),
-                                  in_=vec.rearrange("(c t r) -> t c r", t=PACK, r=4))
+                nc.sync.dma_start(out=raw[Z_PASSES * i : Z_PASSES * (i + 1), :], in_=vec.rearrange("(G c) -> G c", G=Z_PASSES))
 
         def load_contrast():
             gain = kept(("contrast",), [P, HALVES * TILES], BF16)
             nc.sync.dma_start(out=gain[:], in_=contrast.rearrange("(p j) -> p j", p=P))
 
         def widen_channel_rows():
-            nc.vector.tensor_copy(out=tiles[("chrows",)][0 : 2 * PACK, :], in_=tiles[("chraw",)][0 : 2 * PACK, :])
+            live = slice(0, 2 * Z_PASSES)
+            nc.scalar.activation(out=tiles[("chrows",)][live, :].rearrange("k (t a r) -> k t a r", t=PACK, r=4),
+                                 in_=tiles[("chraw",)][live, :].rearrange("k (a t r) -> k t a r", t=PACK, r=4), func=ACT.Identity)
 
         def turn_channel_rows(number):
             acc = bank(("chT",), number)
-            for G in range(Z_PASSES):
-                nc.tensor.transpose(acc[:, G * P : (G + 1) * P], tiles[("chrows",)][:, G * P : (G + 1) * P], ident[:])
+            for t in range(PACK):
+                nc.tensor.transpose(acc[:, t * P : (t + 1) * P], tiles[("chrows",)][:, t * P : (t + 1) * P], ident[:])
 
         def read_channel_columns():
-            acc = tiles[("chT",)][:, 0 : Z_PASSES * P].rearrange("p (G c) -> p G c", G=Z_PASSES)
+            acc = tiles[("chT",)][:].rearrange("p (t k) -> p k t", t=PACK)
             step = kept(("step",), [P, Z_PASSES, PACK], F32)
-            nc.vector.tensor_copy(out=step[:], in_=acc[:, :, PACK : 2 * PACK])
+            nc.vector.tensor_copy(out=step[:], in_=acc[:, Z_PASSES : 2 * Z_PASSES, :])
             shift = kept(("shift",), [P, Z_PASSES, PACK], F32)
-            nc.vector.tensor_tensor(out=shift[:], in0=acc[:, :, 0:PACK], in1=step[:], op=ALU.mult)
+            nc.vector.tensor_tensor(out=shift[:], in0=acc[:, 0:Z_PASSES, :], in1=step[:], op=ALU.mult)
+
+        def spread_mean(number):
+            words = tiles[("meanrows",)][:].bitcast(F32)
+            for b in range(2):
+                acc = bank(("meanT", b), number + b)
+                for w in range(4):
+                    column = words[:, 4 * b + w : 4 * b + w + 1].to_broadcast([P, P])
+                    nc.tensor.transpose(acc[:, w * P : (w + 1) * P], column, ident[:])
+
+        def drain_mean():
+            row = kept(("mean",), [P, PIX], BF16)
+            words = row[:].bitcast(F32).rearrange("p (n w) -> p n w", n=P)
+            for b in range(2):
+                nc.scalar.copy(out=words[:, :, 4 * b : 4 * b + 4], in_=tiles[("meanT", b)][:].rearrange("p (w n) -> p n w", w=4))
 
         def sort_wa(g):
             codes = kept(("wa", g), [P, 2 * C], U8)
@@ -234,31 +249,32 @@ def tile_latent_patch_codec_s9_kernel(tc, x, wa_words, wa_scales, ba, inv_step, 
         make_identity(nc, ident[:])
 
         def make_warm_operands():
-            zeros = kept(("zeros",), [P, P], BF16)
-            codes = kept(("warmq",), [P, N + P], U32)
-            plane = kept(("warms",), [P, N + P], U8)
-            nc.vector.memset(zeros[:], 0.0)
-            nc.vector.memset(codes[:], 0)
-            nc.vector.memset(plane[:].bitcast(U32), 0)
-            nc.vector.quantize_mx(out=codes[:, 0:32].bitcast(E4M3), scales=plane[:, 0:32], in_=zeros[:])
-            nc.vector.quantize_mx(out=codes[:, N : N + 32].bitcast(E5M2), scales=plane[:, N : N + 32], in_=zeros[:])
+            words = kept(("warm",), [P, N + P + (N + P) // 4 + P // 2], U32)
+            nc.vector.memset(words[:], 0)
+            tiles[("warmq",)] = words[:, 0 : N + P]
+            tiles[("warms",)] = words[:, N + P : N + P + (N + P) // 4].bitcast(U8)
+            zeros = words[:, N + P + (N + P) // 4 :].bitcast(BF16)
+            codes, plane = tiles[("warmq",)], tiles[("warms",)]
+            nc.vector.quantize_mx(out=codes[:, 0:32].bitcast(E4M3), scales=plane[:, 0:32], in_=zeros)
+            nc.vector.quantize_mx(out=codes[:, N : N + 32].bitcast(E5M2), scales=plane[:, N : N + 32], in_=zeros)
 
         def warm(count, first):
             codes, plane = tiles[("warmq",)], tiles[("warms",)]
             for i in range(count):
-                acc = bank(("warm", first + i), i % 4)
+                acc = bank(("warm", first + i), (first + i) % 3)
                 nc.tensor.matmul_mx(out=acc[:], lhsT=codes[:, N : N + P].bitcast(E5M2), lhsT_scale=plane[:, N : N + P],
                                     rhs=codes[:, 0:N].bitcast(E4M3), rhs_scale=plane[:, 0:N], start=True, stop=True)
 
-        nc.gpsimd.memset(kept(("chrows",), [P, Z_PASSES * P], F32)[:], 0.0)
+        nc.gpsimd.memset(kept(("chrows",), [P, K_PASS], F32)[:], 0.0)
         load_x(0, 0, 1)
-        load_wa_scales()
-        make_warm_operands()
+        load_channel_rows()
+        load_mean()
         load_wa(0)
         load_x(0, 1, 1)
+        make_warm_operands()
+        load_wa_scales()
         load_wa(1)
         load_x(0, 2, 1)
-        load_channel_rows()
         load_wa(2)
         load_x(0, 3, 1)
         load_wa(3)
@@ -267,7 +283,6 @@ def tile_latent_patch_codec_s9_kernel(tc, x, wa_words, wa_scales, ba, inv_step, 
         load_ws(1, 0)
         load_x(1, 2, 2)
         load_contrast()
-        load_mean()
         load_ws(0, 1)
         load_ws(1, 1)
 
@@ -279,47 +294,49 @@ def tile_latent_patch_codec_s9_kernel(tc, x, wa_words, wa_scales, ba, inv_step, 
             for t in range(PACK):
                 analysis_pass(h, G, t, g, number + t)
 
-        warm(3, 0)
+        warm(4, 0)
         turn_x(0, 0, 4)
         warm(2, 4)
-        sort_wa_scales(0, 1)
         sort_wa(0)
         drain_both(0, 0, "scalar", "vector")
+        widen_channel_rows()
         turn_x(0, 1, 6)
+        turn_channel_rows(3)
+        spread_mean(4)
         quant_x(0, 0)
+        sort_wa_scales(0, 1)
+        read_channel_columns()
         drain_both(0, 1)
+        drain_mean()
         sort_wa_scales(1, 3)
         sort_wa(1)
         wide(0, 0, 0, 0)
         quant_x(0, 1)
-        turn_x(0, 2, 4)
+        turn_x(0, 2, 6)
         drain_both(0, 2)
         sort_wa(2)
-        widen_channel_rows()
         wide(0, 0, 1, 0)
         sort_wa(3)
         quant_x(0, 2)
-        turn_x(0, 3, 6)
-        turn_channel_rows(4)
+        turn_x(0, 3, 4)
         drain_both(0, 3)
         weave_ws(0, 0, "vector", (0,))
         wide(0, 0, 2, 0)
         for g in range(3):
-            analysis_pass(0, 1, 0, g, 5)
+            analysis_pass(0, 1, 0, g, 6)
         quant_x(0, 3)
         weave_ws(0, 0, "vector", (1,))
-        read_channel_columns()
         wide(0, 0, 3, 0)
-        analysis_pass(0, 1, 0, 3, 5)
+        analysis_pass(0, 1, 0, 3, 6)
         weave_ws(0, 1, "scalar", (0,))
         weave_ws(0, 1, "vector", (1,))
         quant_ws(0, 0)
         for t in range(PACK):
             drain_y(0, 0, t)
         quant_ws(0, 1)
-        analysis(0, 1, 1, 6)
-        turn_x(1, 0, 7)
-        analysis(0, 1, 2, 4)
+        analysis(0, 1, 1, 7)
+        turn_x(1, 0, 4)
+        analysis(0, 1, 2, 0)
         analysis(0, 1, 3, 1)
         weave_ws(1, 0, "vector")
         weave_z(0, 0, "vector")

@@ -62,11 +62,14 @@ def tile_latent_patch_codec_s9_kernel(tc, x, wa_words, wa_scales, ba, inv_step, 
             else:
                 nc.vector.tensor_copy(out=dst, in_=src)
 
-        def load_x(h, g0, count):
-            raw = kept(("xraw", h, g0), [P, TILES, count * K_PASS], BF16)
-            nc.sync.dma_start(out=raw[:], in_=x_rows[h, :, :, g0 * K_PASS : (g0 + count) * K_PASS])
-            for g in range(g0, g0 + count):
-                tiles[("xwords", h, g)] = raw[:].bitcast(F32)[:, :, (g - g0) * 256 : (g - g0 + 1) * 256]
+        def load_x(h, g0, count, halves=1):
+            rows = TILES // halves
+            for part in range(halves):
+                raw = kept(("xraw", h, g0, part), [P, rows, count * K_PASS], BF16)
+                nc.sync.dma_start(out=raw[:], in_=x_rows[h, :, part * rows : (part + 1) * rows, g0 * K_PASS : (g0 + count) * K_PASS])
+                for g in range(g0, g0 + count):
+                    for j in range(rows):
+                        tiles[("xwords", h, g, part * rows + j)] = raw[:].bitcast(F32)[:, j, (g - g0) * 256 : (g - g0 + 1) * 256]
 
         def load_wa(g):
             raw = kept(("waraw", g), [P, C // 2], I32)
@@ -79,14 +82,18 @@ def tile_latent_patch_codec_s9_kernel(tc, x, wa_words, wa_scales, ba, inv_step, 
                 nc.sync.dma_start(out=raw[32 * q : 32 * q + 4, :, :],
                                   in_=wa_scales[:, 4 * q : 4 * q + 4, :].rearrange("g r n -> r g n").bitcast(I32))
 
-        def load_ws(G, w):
-            raw = kept(("wsraw", G, w), [P, PACK, WS_WIDTH], BF16)
+        def load_ws(G, first, count):
+            raw = kept(("wsraw", G, first), [P, PACK, count * N], BF16)
             for r in range(4):
-                nc.sync.dma_start(out=raw[r:P:4, :, :], in_=ws_rows[G, r, :, :, w * WS_WIDTH : (w + 1) * WS_WIDTH])
+                nc.sync.dma_start(out=raw[r:P:4, :, :], in_=ws_rows[G, r, :, :, first * N : (first + count) * N])
+            for n in range(first, first + count):
+                tiles[("wsrows", G, n)] = raw[:, :, (n - first) * N : (n - first + 1) * N]
 
-        def load_mean():
-            rows = kept(("meanrows",), [P, PIX // P], BF16)
-            nc.sync.dma_start(out=rows[:], in_=mean.rearrange("(n w) -> n w", n=P))
+        def load_mean(first, count):
+            row = kept(("meanrow", first), [P, count * N], BF16)
+            nc.sync.dma_start(out=row[:], in_=mean[first * N : (first + count) * N].partition_broadcast(P))
+            for n in range(first, first + count):
+                tiles[("mean", n)] = row[:, (n - first) * N : (n - first + 1) * N]
 
         def load_channel_rows():
             raw = kept(("chraw",), [P, K_PASS], BF16)
@@ -114,19 +121,6 @@ def tile_latent_patch_codec_s9_kernel(tc, x, wa_words, wa_scales, ba, inv_step, 
             shift = kept(("shift",), [P, Z_PASSES, PACK], F32)
             nc.vector.tensor_tensor(out=shift[:], in0=acc[:, 0:Z_PASSES, :], in1=step[:], op=ALU.mult)
 
-        def spread_mean(number):
-            words = tiles[("meanrows",)][:].bitcast(F32)
-            for b in range(2):
-                acc = bank(("meanT", b), number + b)
-                for w in range(4):
-                    column = words[:, 4 * b + w : 4 * b + w + 1].to_broadcast([P, P])
-                    nc.tensor.transpose(acc[:, w * P : (w + 1) * P], column, ident[:])
-
-        def drain_mean():
-            row = kept(("mean",), [P, PIX], BF16)
-            words = row[:].bitcast(F32).rearrange("p (n w) -> p n w", n=P)
-            for b in range(2):
-                nc.scalar.copy(out=words[:, :, 4 * b : 4 * b + 4], in_=tiles[("meanT", b)][:].rearrange("p (w n) -> p n w", w=4))
 
         def sort_wa(g):
             codes = kept(("wa", g), [P, 2 * C], U8)
@@ -143,13 +137,12 @@ def tile_latent_patch_codec_s9_kernel(tc, x, wa_words, wa_scales, ba, inv_step, 
                 in_=tiles[("scraw",)][:, g0 : g0 + count, :].rearrange("p g (c i t) -> p g c t i", t=PACK, i=4))
 
         def turn_x(h, g, number):
-            words = tiles[("xwords", h, g)]
             for b in range(2):
                 acc = bank(("xT", h, g, b), number + b)
                 for jj in range(2):
                     for u in range(2):
                         s = 2 * jj + u
-                        nc.tensor.transpose(acc[:, s * P : (s + 1) * P], words[:, 2 * b + jj, u::2], ident[:])
+                        nc.tensor.transpose(acc[:, s * P : (s + 1) * P], tiles[("xwords", h, g, 2 * b + jj)][:, u::2], ident[:])
 
         def drain_x(h, g, b, engine):
             if b == 0:
@@ -205,8 +198,7 @@ def tile_latent_patch_codec_s9_kernel(tc, x, wa_words, wa_scales, ba, inv_step, 
             quantize(("z", h, G), tiles[("woven", "z", h, G)][:], E5M2, parts)
 
         def weave_ws(G, n, engine, parts=(0, 1)):
-            w, part = divmod(n, WS_WIDTH // N)
-            weave(("ws", G, n), tiles[("wsraw", G, w)][:, :, part * N : (part + 1) * N], engine, parts)
+            weave(("ws", G, n), tiles[("wsrows", G, n)], engine, parts)
 
         def quant_ws(G, n):
             quantize(("ws", G, n), tiles[("woven", "ws", G, n)][:], E4M3)
@@ -227,11 +219,11 @@ def tile_latent_patch_codec_s9_kernel(tc, x, wa_words, wa_scales, ba, inv_step, 
 
         def finish(h, j, n, first, count, aside):
             if n == first:
-                staged(("res", h, j, first), [P, count * N], F32, 6)
+                staged(("res", h, j, first), [P, count * N], F32, 8)
             res = tiles[("res", h, j, first)][:, (n - first) * N : (n - first + 1) * N]
             row = h * TILES + j
             gain = tiles[("gain",)][:, row : row + 1]
-            shift = tiles[("mean",)][:, n * N : (n + 1) * N]
+            shift = tiles[("mean", n)]
             if aside:
                 nc.scalar.activation(out=res, in_=tiles[("r", h, j, n)][:], func=ACT.Copy, scale=gain)
                 nc.gpsimd.tensor_tensor(out=res, in0=res, in1=shift, op=ALU.add)
@@ -268,7 +260,6 @@ def tile_latent_patch_codec_s9_kernel(tc, x, wa_words, wa_scales, ba, inv_step, 
         nc.gpsimd.memset(kept(("chrows",), [P, K_PASS], F32)[:], 0.0)
         load_x(0, 0, 1)
         load_channel_rows()
-        load_mean()
         load_wa(0)
         load_x(0, 1, 1)
         make_warm_operands()
@@ -276,15 +267,19 @@ def tile_latent_patch_codec_s9_kernel(tc, x, wa_words, wa_scales, ba, inv_step, 
         load_wa(1)
         load_x(0, 2, 1)
         load_wa(2)
+        load_ws(0, 0, 1)
         load_x(0, 3, 1)
         load_wa(3)
-        load_ws(0, 0)
+        load_ws(0, 1, 1)
+        load_ws(1, 0, 1)
         load_x(1, 0, 2)
-        load_ws(1, 0)
+        load_ws(1, 1, 1)
         load_x(1, 2, 2)
         load_contrast()
-        load_ws(0, 1)
-        load_ws(1, 1)
+        load_mean(0, 1)
+        load_ws(0, 2, 2)
+        load_ws(1, 2, 2)
+        load_mean(1, 3)
 
         def drain_both(h, g, e0="scalar", e1="scalar"):
             drain_x(h, g, 0, e0)
@@ -301,99 +296,97 @@ def tile_latent_patch_codec_s9_kernel(tc, x, wa_words, wa_scales, ba, inv_step, 
         drain_both(0, 0, "scalar", "vector")
         widen_channel_rows()
         turn_x(0, 1, 6)
-        turn_channel_rows(3)
-        spread_mean(4)
+        turn_channel_rows(4)
         quant_x(0, 0)
         sort_wa_scales(0, 1)
-        read_channel_columns()
         drain_both(0, 1)
-        drain_mean()
-        sort_wa_scales(1, 3)
         sort_wa(1)
+        sort_wa_scales(1, 3)
         wide(0, 0, 0, 0)
         quant_x(0, 1)
+        read_channel_columns()
         turn_x(0, 2, 6)
         drain_both(0, 2)
         sort_wa(2)
         wide(0, 0, 1, 0)
-        sort_wa(3)
+        weave_ws(0, 0, "vector", (0,))
         quant_x(0, 2)
+        weave_ws(0, 0, "vector", (1,))
         turn_x(0, 3, 4)
         drain_both(0, 3)
-        weave_ws(0, 0, "vector", (0,))
+        sort_wa(3)
+        quant_ws(0, 0)
         wide(0, 0, 2, 0)
         for g in range(3):
             analysis_pass(0, 1, 0, g, 6)
         quant_x(0, 3)
-        weave_ws(0, 0, "vector", (1,))
-        wide(0, 0, 3, 0)
-        analysis_pass(0, 1, 0, 3, 6)
         weave_ws(0, 1, "scalar", (0,))
         weave_ws(0, 1, "vector", (1,))
-        quant_ws(0, 0)
+        wide(0, 0, 3, 0)
+        analysis_pass(0, 1, 0, 3, 6)
+        quant_ws(0, 1)
+        weave_ws(1, 0, "vector")
         for t in range(PACK):
             drain_y(0, 0, t)
-        quant_ws(0, 1)
         analysis(0, 1, 1, 7)
         turn_x(1, 0, 4)
         analysis(0, 1, 2, 0)
         analysis(0, 1, 3, 1)
-        weave_ws(1, 0, "vector")
-        weave_z(0, 0, "vector")
-        drain_y(0, 1, 0)
-        drain_both(1, 0)
-        drain_y(0, 1, 1)
         quant_ws(1, 0)
+        drain_x(1, 0, 0, "vector")
+        weave_z(0, 0, "vector")
+        drain_x(1, 0, 1, "scalar")
+        drain_y(0, 1, 0)
+        drain_y(0, 1, 1)
         quant_x(1, 0)
         quant_z(0, 0)
-        weave_ws(1, 1, "vector", (0,))
         turn_x(1, 1, 2)
         drain_y(0, 1, 2)
         drain_y(0, 1, 3)
-        drain_both(1, 1)
+        drain_both(1, 1, "vector", "scalar")
         wide(1, 0, 0, 4)
-        weave_z(0, 1, "vector")
         quant_x(1, 1)
-        quant_z(0, 1)
-        weave_ws(1, 1, "scalar", (1,))
+        weave_z(0, 1, "vector")
+        weave_ws(1, 1, "scalar", (0,))
         turn_x(1, 2, 0)
         drain_both(1, 2)
         wide(1, 0, 1, 4)
-        quant_ws(1, 1)
         widen_contrast()
+        quant_z(0, 1)
         quant_x(1, 2)
-        weave_ws(0, 2, "vector")
-        weave_ws(1, 2, "scalar", (0,))
+        weave_ws(1, 1, "vector", (1,))
         turn_x(1, 3, 2)
         drain_both(1, 3)
+        weave_ws(1, 2, "scalar")
         synthesis(0, 0, 0, 0)
         synthesis(0, 1, 0, 1)
         wide(1, 0, 2, 4)
-        weave_ws(1, 2, "scalar", (1,))
         quant_x(1, 3)
-        quant_ws(0, 2)
-        weave_ws(0, 3, "scalar")
+        quant_ws(1, 1)
         synthesis(0, 2, 0, 2)
         synthesis(0, 3, 0, 3)
         wide(1, 0, 3, 4)
-        quant_ws(1, 2)
+        weave_ws(0, 2, "vector")
         for t in range(PACK):
             drain_y(1, 0, t)
+        weave_ws(0, 3, "scalar")
         synthesis(0, 0, 1, 0)
         synthesis(0, 1, 1, 1)
-        quant_ws(0, 3)
-        synthesis(0, 2, 1, 2)
-        synthesis(0, 3, 1, 3)
-        weave_ws(1, 3, "scalar", (0,))
-        analysis(1, 1, 0, 4)
-        weave_z(1, 0, "vector")
+        quant_ws(0, 2)
+        quant_ws(1, 2)
+        analysis(1, 1, 0, 2)
         drain_y(1, 1, 0)
-        weave_ws(1, 3, "scalar", (1,))
+        synthesis(0, 2, 1, 3)
+        synthesis(0, 3, 1, 4)
+        weave_ws(1, 3, "scalar", (0,))
+        weave_z(1, 0, "vector")
         synthesis(0, 0, 2, 5)
         quant_z(1, 0)
         synthesis(0, 1, 2, 6)
         analysis(1, 1, 1, 7)
         drain_y(1, 1, 1)
+        weave_ws(1, 3, "scalar", (1,))
+        quant_ws(0, 3)
         synthesis(0, 2, 2, 0)
         quant_ws(1, 3)
         analysis(1, 1, 2, 1)
@@ -413,8 +406,8 @@ def tile_latent_patch_codec_s9_kernel(tc, x, wa_words, wa_scales, ba, inv_step, 
         number = 0
         for j in range(TILES):
             for n in range(OUT_CHUNKS):
-                if j == TILES - 1 and n >= 2:
-                    synthesis(1, j, n, number)
+                if (j == 3 and n >= 2):
+                    synthesis(1, j, n, number, aside=(n == 0 and j < 3))
                 else:
-                    synthesis(1, j, n, number, first=n - n % 2, count=2, aside=False)
+                    synthesis(1, j, n, number, first=n - n % 2, count=2, aside=(n == 0 and j < 3))
                 number = number + 1

from contextlib import ExitStack

import concourse.mybir as mybir
from concourse.masks import make_identity

M, PIX, C = 1024, 2048, 1024
FLOPS = 2 * M * PIX * C * 2

F32 = mybir.dt.float32
BF16 = mybir.dt.bfloat16
I32 = mybir.dt.int32
U32 = mybir.dt.uint32
U8 = mybir.dt.uint8
E4M3 = mybir.dt.float8_e4m3fn_x4
E5M2 = mybir.dt.float8_e5m2_x4
E2M1 = mybir.dt.float4_e2m1fn_x4
ALU = mybir.AluOpType
ACT = mybir.ActivationFunctionType

P = 128
PACK = 4
K_PASS = P * PACK
N = 512
X_PASSES = PIX // K_PASS
Z_PASSES = C // K_PASS
HALVES = M // N
TILES = N // P
OUT_CHUNKS = PIX // N
WS_WIDTH = 2 * N
BANKS = 8


def tile_latent_patch_codec_s9_kernel(tc, x, wa_words, wa_scales, ba, inv_step, ws, contrast, mean, out):
    nc = tc.nc
    x_rows = x.rearrange("(p h j) k -> h p j k", h=HALVES, j=TILES)
    out_rows = out.rearrange("(p h j) n -> h j p n", h=HALVES, j=TILES)
    ws_rows = ws.rearrange("(G a t r) n -> G r a t n", G=Z_PASSES, t=PACK, r=4)

    with ExitStack() as ctx:
        keep = ctx.enter_context(tc.tile_pool(name="keep", bufs=1))
        stage = ctx.enter_context(tc.tile_pool(name="stage", bufs=3))
        psum = ctx.enter_context(tc.psum_pool(name="psum", bufs=1))
        ctx.enter_context(tc.manual_schedule())

        tiles = {}

        def kept(key, shape, dtype):
            tiles[key] = keep.tile(shape, dtype, name="k" + "x".join([str(part) for part in key]), align_bytes=64)
            return tiles[key]

        def staged(key, shape, dtype, bufs):
            tiles[key] = stage.tile(shape, dtype, name="s" + "x".join([str(part) for part in key]), tag=key[0], bufs=bufs, align_bytes=64)
            return tiles[key]

        def bank(key, number):
            tiles[key] = psum.tile([P, N], F32, name="b" + "x".join([str(part) for part in key]), tag="bank%d" % (number % BANKS))
            return tiles[key]

        def copy_on(engine, dst, src):
            if engine == "scalar":
                nc.scalar.copy(out=dst, in_=src)
            else:
                nc.vector.tensor_copy(out=dst, in_=src)

        def load_x(h, g0, count, halves=1):
            rows = TILES // halves
            for part in range(halves):
                raw = kept(("xraw", h, g0, part), [P, rows, count * K_PASS], BF16)
                nc.sync.dma_start(out=raw[:], in_=x_rows[h, :, part * rows : (part + 1) * rows, g0 * K_PASS : (g0 + count) * K_PASS])
                for g in range(g0, g0 + count):
                    for j in range(rows):
                        tiles[("xwords", h, g, part * rows + j)] = raw[:].bitcast(F32)[:, j, (g - g0) * 256 : (g - g0 + 1) * 256]

        def load_wa(g):
            raw = kept(("waraw", g), [P, C // 2], I32)
            nc.sync.dma_start(out=raw[:], in_=wa_words[g].bitcast(I32))

        def load_wa_scales():
            raw = kept(("scraw",), [P, X_PASSES, C // 4], I32)
            nc.vector.memset(raw[:], 0)
            for q in range(4):
                nc.sync.dma_start(out=raw[32 * q : 32 * q + 4, :, :],
                                  in_=wa_scales[:, 4 * q : 4 * q + 4, :].rearrange("g r n -> r g n").bitcast(I32))

        def load_ws(G, first, count):
            raw = kept(("wsraw", G, first), [P, PACK, count * N], BF16)
            for r in range(4):
                nc.sync.dma_start(out=raw[r:P:4, :, :], in_=ws_rows[G, r, :, :, first * N : (first + count) * N])
            for n in range(first, first + count):
                tiles[("wsrows", G, n)] = raw[:, :, (n - first) * N : (n - first + 1) * N]

        def load_mean(first, count):
            row = kept(("meanrow", first), [P, count * N], BF16)
            nc.sync.dma_start(out=row[:], in_=mean[first * N : (first + count) * N].partition_broadcast(P))
            for n in range(first, first + count):
                tiles[("mean", n)] = row[:, (n - first) * N : (n - first + 1) * N]

        def load_channel_rows():
            raw = kept(("chraw",), [P, K_PASS], BF16)
            for i, vec in enumerate((ba, inv_step)):
                nc.sync.dma_start(out=raw[Z_PASSES * i : Z_PASSES * (i + 1), :], in_=vec.rearrange("(G c) -> G c", G=Z_PASSES))

        def load_contrast():
            gain = kept(("contrast",), [P, HALVES * TILES], BF16)
            nc.sync.dma_start(out=gain[:], in_=contrast.rearrange("(p j) -> p j", p=P))

        def widen_channel_rows():
            live = slice(0, 2 * Z_PASSES)
            nc.scalar.activation(out=tiles[("chrows",)][live, :].rearrange("k (t a r) -> k t a r", t=PACK, r=4),
                                 in_=tiles[("chraw",)][live, :].rearrange("k (a t r) -> k t a r", t=PACK, r=4), func=ACT.Identity)

        def turn_channel_rows(number):
            acc = bank(("chT",), number)
            for t in range(PACK):
                nc.tensor.transpose(acc[:, t * P : (t + 1) * P], tiles[("chrows",)][:, t * P : (t + 1) * P], ident[:])

        def read_channel_columns():
            acc = tiles[("chT",)][:].rearrange("p (t k) -> p k t", t=PACK)
            step = kept(("step",), [P, Z_PASSES, PACK], F32)
            nc.vector.tensor_copy(out=step[:], in_=acc[:, Z_PASSES : 2 * Z_PASSES, :])
            shift = kept(("shift",), [P, Z_PASSES, PACK], F32)
            nc.vector.tensor_tensor(out=shift[:], in0=acc[:, 0:Z_PASSES, :], in1=step[:], op=ALU.mult)


        def sort_wa(g):
            codes = kept(("wa", g), [P, 2 * C], U8)
            nc.vector.tensor_copy(
                out=codes[:].bitcast(I32).rearrange("p (t c a e) -> p c t a e", t=PACK, a=2, e=2),
                in_=tiles[("waraw", g)][:].rearrange("p (c a t e) -> p c t a e", t=PACK, a=2, e=2))

        def sort_wa_scales(g0, count):
            if g0 == 0:
                kept(("wasc",), [P, X_PASSES * C], U8)
            words = tiles[("wasc",)][:].bitcast(I32)[:, g0 * (C // 4) : (g0 + count) * (C // 4)]
            nc.vector.tensor_copy(
                out=words.rearrange("p (g t c i) -> p g c t i", g=count, t=PACK, i=4),
                in_=tiles[("scraw",)][:, g0 : g0 + count, :].rearrange("p g (c i t) -> p g c t i", t=PACK, i=4))

        def turn_x(h, g, number):
            for b in range(2):
                acc = bank(("xT", h, g, b), number + b)
                for jj in range(2):
                    for u in range(2):
                        s = 2 * jj + u
                        nc.tensor.transpose(acc[:, s * P : (s + 1) * P], tiles[("xwords", h, g, 2 * b + jj)][:, u::2], ident[:])

        def drain_x(h, g, b, engine):
            if b == 0:
                staged(("xg", h, g), [P, PACK * N], BF16, 3)
            dst = tiles[("xg", h, g)][:].bitcast(F32)[:, b * N : (b + 1) * N].rearrange("p (j m u) -> p j m u", j=2, u=2)
            copy_on(engine, dst, tiles[("xT", h, g, b)][:].rearrange("p (j u m) -> p j m u", j=2, u=2))

        def quantize(key, src, fmt, parts=(0, 1)):
            if parts[0] == 0:
                kept(key + ("q",), [P, N], U32)
                kept(key + ("s",), [P, N], U8)
            lo, hi = parts[0] * (N // 2), (parts[-1] + 1) * (N // 2)
            nc.vector.quantize_mx(out=tiles[key + ("q",)][:, lo:hi].bitcast(fmt), scales=tiles[key + ("s",)][:, lo:hi],
                                  in_=src[:, PACK * lo : PACK * hi])

        def quant_x(h, g):
            quantize(("x", h, g), tiles[("xg", h, g)][:], E4M3)

        def analysis_pass(h, G, t, g, number):
            if g == 0:
                bank(("y", h, G, t), number)
            col = (t * Z_PASSES + G) * P
            nc.tensor.matmul_mx(
                out=tiles[("y", h, G, t)][:],
                lhsT=tiles[("wa", g)][:, 2 * col : 2 * (col + P)].bitcast(E2M1),
                lhsT_scale=tiles[("wasc",)][:, g * C + col : g * C + col + P],
                rhs=tiles[("x", h, g, "q")][:].bitcast(E4M3),
                rhs_scale=tiles[("x", h, g, "s")][:],
                start=(g == 0), stop=(g == X_PASSES - 1))

        def analysis(h, G, t, number):
            for g in range(X_PASSES):
                analysis_pass(h, G, t, g, number)

        def drain_y(h, G, t, parts=(0, 1)):
            if t == 0:
                staged(("zrows", h, G), [P, PACK, N], BF16, 2)
            cols = slice(parts[0] * (N // 2), (parts[-1] + 1) * (N // 2))
            nc.scalar.activation(out=tiles[("zrows", h, G)][:, t, cols], in_=tiles[("y", h, G, t)][:, cols], func=ACT.Identity,
                                 bias=tiles[("shift",)][:, G, t : t + 1], scale=tiles[("step",)][:, G, t : t + 1])

        def weave(key, src, engine, parts):
            if ("woven",) + key not in tiles:
                staged(("woven",) + key, [P, PACK * N], BF16, 4)
            cols = slice(parts[0] * (N // 2), (parts[-1] + 1) * (N // 2))
            dst = tiles[("woven",) + key][:].rearrange("p (n t) -> p n t", t=PACK)[:, cols, :]
            copy_on(engine, dst.rearrange("p (c i) t -> p c t i", i=4), src[:, :, cols].rearrange("p t (c i) -> p c t i", i=4))

        def weave_z(h, G, engine, parts=(0, 1)):
            weave(("z", h, G), tiles[("zrows", h, G)][:], engine, parts)

        def quant_z(h, G, parts=(0, 1)):
            quantize(("z", h, G), tiles[("woven", "z", h, G)][:], E5M2, parts)

        def weave_ws(G, n, engine, parts=(0, 1)):
            weave(("ws", G, n), tiles[("wsrows", G, n)], engine, parts)

        def quant_ws(G, n):
            quantize(("ws", G, n), tiles[("woven", "ws", G, n)][:], E4M3)

        def synthesis_pass(h, j, n, G, number):
            if G == 0:
                bank(("r", h, j, n), number)
            nc.tensor.matmul_mx(
                out=tiles[("r", h, j, n)][:],
                lhsT=tiles[("z", h, G, "q")][:, j * P : (j + 1) * P].bitcast(E5M2),
                lhsT_scale=tiles[("z", h, G, "s")][:, j * P : (j + 1) * P],
                rhs=tiles[("ws", G, n, "q")][:].bitcast(E4M3),
                rhs_scale=tiles[("ws", G, n, "s")][:],
                start=(G == 0), stop=(G == Z_PASSES - 1))

        def widen_contrast():
            nc.vector.tensor_copy(out=kept(("gain",), [P, HALVES * TILES], F32)[:], in_=tiles[("contrast",)][:])

        def finish(h, j, n, first, count, aside):
            if n == first:
                staged(("res", h, j, first), [P, count * N], F32, 8)
            res = tiles[("res", h, j, first)][:, (n - first) * N : (n - first + 1) * N]
            row = h * TILES + j
            gain = tiles[("gain",)][:, row : row + 1]
            shift = tiles[("mean", n)]
            if aside:
                nc.scalar.activation(out=res, in_=tiles[("r", h, j, n)][:], func=ACT.Copy, scale=gain)
                nc.gpsimd.tensor_tensor(out=res, in0=res, in1=shift, op=ALU.add)
            else:
                nc.vector.scalar_tensor_tensor(out=res, in0=tiles[("r", h, j, n)][:], scalar=gain, in1=shift, op0=ALU.mult, op1=ALU.add)
            if n == first + count - 1:
                nc.sync.dma_start(out=out_rows[h, j, :, first * N : (first + count) * N], in_=tiles[("res", h, j, first)][:])

        def synthesis(h, j, n, number, first=None, count=1, aside=False):
            for G in range(Z_PASSES):
                synthesis_pass(h, j, n, G, number)
            finish(h, j, n, n if first is None else first, count, aside)

        ident = kept(("ident",), [P, P], F32)
        make_identity(nc, ident[:])

        def make_warm_operands():
            words = kept(("warm",), [P, N + P + (N + P) // 4 + P // 2], U32)
            nc.vector.memset(words[:], 0)
            tiles[("warmq",)] = words[:, 0 : N + P]
            tiles[("warms",)] = words[:, N + P : N + P + (N + P) // 4].bitcast(U8)
            zeros = words[:, N + P + (N + P) // 4 :].bitcast(BF16)
            codes, plane = tiles[("warmq",)], tiles[("warms",)]
            nc.vector.quantize_mx(out=codes[:, 0:32].bitcast(E4M3), scales=plane[:, 0:32], in_=zeros)
            nc.vector.quantize_mx(out=codes[:, N : N + 32].bitcast(E5M2), scales=plane[:, N : N + 32], in_=zeros)

        def warm(count, first):
            codes, plane = tiles[("warmq",)], tiles[("warms",)]
            for i in range(count):
                acc = bank(("warm", first + i), (first + i) % 3)
                nc.tensor.matmul_mx(out=acc[:], lhsT=codes[:, N : N + P].bitcast(E5M2), lhsT_scale=plane[:, N : N + P],
                                    rhs=codes[:, 0:N].bitcast(E4M3), rhs_scale=plane[:, 0:N], start=True, stop=True)

        nc.gpsimd.memset(kept(("chrows",), [P, K_PASS], F32)[:], 0.0)
        load_x(0, 0, 1)
        load_channel_rows()
        load_wa(0)
        load_x(0, 1, 1)
        make_warm_operands()
        load_wa_scales()
        load_wa(1)
        load_x(0, 2, 1)
        load_wa(2)
        load_ws(0, 0, 1)
        load_x(0, 3, 1)
        load_wa(3)
        load_ws(0, 1, 1)
        load_ws(1, 0, 1)
        load_x(1, 0, 2)
        load_ws(1, 1, 1)
        load_x(1, 2, 2)
        load_contrast()
        load_mean(0, 1)
        load_ws(0, 2, 2)
        load_ws(1, 2, 2)
        load_mean(1, 3)

        def drain_both(h, g, e0="scalar", e1="scalar"):
            drain_x(h, g, 0, e0)
            drain_x(h, g, 1, e1)

        def wide(h, G, g, number):
            for t in range(PACK):
                analysis_pass(h, G, t, g, number + t)

        warm(4, 0)
        turn_x(0, 0, 4)
        warm(2, 4)
        sort_wa(0)
        drain_both(0, 0, "scalar", "vector")
        widen_channel_rows()
        turn_x(0, 1, 6)
        turn_channel_rows(4)
        quant_x(0, 0)
        sort_wa_scales(0, 1)
        drain_both(0, 1)
        sort_wa(1)
        sort_wa_scales(1, 3)
        wide(0, 0, 0, 0)
        quant_x(0, 1)
        read_channel_columns()
        turn_x(0, 2, 6)
        drain_both(0, 2)
        sort_wa(2)
        wide(0, 0, 1, 0)
        weave_ws(0, 0, "vector", (0,))
        quant_x(0, 2)
        weave_ws(0, 0, "vector", (1,))
        turn_x(0, 3, 4)
        drain_both(0, 3)
        sort_wa(3)
        quant_ws(0, 0)
        wide(0, 0, 2, 0)
        for g in range(3):
            analysis_pass(0, 1, 0, g, 6)
        quant_x(0, 3)
        weave_ws(0, 1, "scalar", (0,))
        weave_ws(0, 1, "vector", (1,))
        wide(0, 0, 3, 0)
        analysis_pass(0, 1, 0, 3, 6)
        quant_ws(0, 1)
        weave_ws(1, 0, "vector")
        for t in range(PACK):
            drain_y(0, 0, t)
        analysis(0, 1, 1, 7)
        turn_x(1, 0, 4)
        analysis(0, 1, 2, 0)
        analysis(0, 1, 3, 1)
        quant_ws(1, 0)
        drain_x(1, 0, 0, "vector")
        weave_z(0, 0, "vector")
        drain_x(1, 0, 1, "scalar")
        drain_y(0, 1, 0)
        drain_y(0, 1, 1)
        quant_x(1, 0)
        quant_z(0, 0)
        turn_x(1, 1, 2)
        drain_y(0, 1, 2)
        drain_y(0, 1, 3)
        drain_both(1, 1, "vector", "scalar")
        wide(1, 0, 0, 4)
        quant_x(1, 1)
        weave_z(0, 1, "vector")
        weave_ws(1, 1, "scalar", (0,))
        turn_x(1, 2, 0)
        drain_both(1, 2)
        wide(1, 0, 1, 4)
        widen_contrast()
        quant_z(0, 1)
        quant_x(1, 2)
        weave_ws(1, 1, "vector", (1,))
        turn_x(1, 3, 2)
        drain_both(1, 3)
        weave_ws(1, 2, "scalar")
        synthesis(0, 0, 0, 0)
        synthesis(0, 1, 0, 1)
        wide(1, 0, 2, 4)
        quant_x(1, 3)
        quant_ws(1, 1)
        synthesis(0, 2, 0, 2)
        synthesis(0, 3, 0, 3)
        wide(1, 0, 3, 4)
        weave_ws(0, 2, "vector")
        for t in range(PACK):
            drain_y(1, 0, t)
        weave_ws(0, 3, "scalar")
        synthesis(0, 0, 1, 0)
        synthesis(0, 1, 1, 1)
        quant_ws(0, 2)
        quant_ws(1, 2)
        analysis(1, 1, 0, 2)
        drain_y(1, 1, 0)
        synthesis(0, 2, 1, 3)
        synthesis(0, 3, 1, 4)
        weave_ws(1, 3, "scalar", (0,))
        weave_z(1, 0, "vector")
        synthesis(0, 0, 2, 5)
        quant_z(1, 0)
        synthesis(0, 1, 2, 6)
        analysis(1, 1, 1, 7)
        drain_y(1, 1, 1)
        weave_ws(1, 3, "scalar", (1,))
        quant_ws(0, 3)
        synthesis(0, 2, 2, 0)
        quant_ws(1, 3)
        analysis(1, 1, 2, 1)
        analysis(1, 1, 3, 2)
        drain_y(1, 1, 2)
        drain_y(1, 1, 3, (0,))
        weave_z(1, 1, "scalar", (0,))
        drain_y(1, 1, 3, (1,))
        weave_z(1, 1, "scalar", (1,))
        synthesis(0, 3, 2, 3)
        synthesis(0, 0, 3, 4)
        synthesis(0, 1, 3, 5)
        quant_z(1, 1, (0,))
        synthesis(0, 2, 3, 6)
        synthesis(0, 3, 3, 7)
        quant_z(1, 1, (1,))
        number = 0
        for j in range(TILES):
            for n in range(OUT_CHUNKS):
                if (j == 3 and n >= 2):
                    synthesis(1, j, n, number, aside=(n == 0 and j < 3))
                else:
                    synthesis(1, j, n, number, first=n - n % 2, count=2, aside=(n == 0 and j < 3))
                number = number + 1
